import numpy as np
import ml_dtypes


def mxq(x, axis, fmt="e4m3"):
    dtype, down = {"e4m3": (ml_dtypes.float8_e4m3fn, 7), "e5m2": (ml_dtypes.float8_e5m2, 14)}[fmt]
    v = np.moveaxis(np.asarray(x, np.float32).astype(ml_dtypes.bfloat16).astype(np.float64), axis, -1)
    blocks = v.reshape(v.shape[:-1] + (-1, 32))
    amax = np.abs(blocks).max(-1, keepdims=True)
    byte = np.maximum(np.where(amax > 0, np.frexp(amax)[1] - 1 + 127, 0) - down, 1)
    scale = np.exp2(byte - 127.0)
    codes = (blocks / scale).astype(np.float32).astype(dtype).astype(np.float64)
    return np.moveaxis((codes * scale).reshape(v.shape), -1, axis)


WIDE = False


def mx_kscale(k):
    if not WIDE:
        return np.ones(k)
    levels = np.array([24, -24, 12, -12, 0])
    if k % 512:
        return np.exp2(np.random.permutation(np.resize(levels, k // 32))).repeat(32)
    a = np.empty((k // 512, 16))
    for p in range(k // 512):
        a[p, :8] = np.random.permutation(np.resize(levels, 8))
        for g in range(8):
            far = levels[np.abs(levels - a[p, g]) >= 10]
            a[p, g + 8] = far[np.random.randint(len(far))]
    return np.exp2(a.ravel()).repeat(32)


def f64(x):
    return np.asarray(x).astype(np.float64)


def striped8(idx):
    return np.concatenate([v.reshape(-1, 16).T for v in idx]).astype(np.uint16)


def unstriped8(offs):
    return np.stack([offs[16 * g:16 * g + 16].T.reshape(-1) for g in range(8)]).astype(np.int64)


E2M1 = np.array([0.0, 0.5, 1.0, 1.5, 2.0, 3.0, 4.0, 6.0, -0.0, -0.5, -1.0, -1.5, -2.0, -3.0, -4.0, -6.0])


def pack_weight(w, fmt):
    k, n = w.shape
    w = f64(np.asarray(w, np.float32).astype(ml_dtypes.bfloat16)).reshape(k // 32, 32, n)
    amax = np.abs(w).max(1)
    if fmt == "e4m3":
        byte = np.frexp(amax)[1] - 1 + 127 - 7
    else:
        mant, ex = np.frexp(amax / 6.0)
        byte = np.where(mant > 0.5, ex, ex - 1) + 127
    byte = np.clip(np.where(amax > 0, byte, 1), 1, 254)
    scaled = (w * np.exp2(127.0 - byte)[:, None, :]).reshape(k, n).astype(np.float32)
    by_word = np.ascontiguousarray(scaled.reshape(k // 512, 128, 4, n).transpose(0, 1, 3, 2))
    if fmt == "e4m3":
        words = by_word.astype(ml_dtypes.float8_e4m3fn).view(np.uint8)
    else:
        c = by_word.astype(ml_dtypes.float4_e2m1fn).view(np.uint8) & 0xF
        words = (c[..., 0::2] | (c[..., 1::2] << 4)).reshape(k // 512, 128, 2 * n)
    return np.ascontiguousarray(words), np.ascontiguousarray(byte.astype(np.uint8).reshape(k // 512, 16, n))


def unpack_weight(words, scales, fmt):
    g, _, n = scales.shape
    words = np.ascontiguousarray(words).reshape(g, 128, n, -1)
    if fmt == "e4m3":
        vals = words.view(ml_dtypes.float8_e4m3fn).astype(np.float64)
    else:
        nib = np.empty((g, 128, n, 4), np.uint8)
        nib[..., 0::2] = words & 0xF
        nib[..., 1::2] = words >> 4
        vals = E2M1[nib]
    vals = vals * np.repeat(np.exp2(scales.astype(np.float64) - 127.0), 8, axis=1)[..., None]
    return vals.transpose(0, 1, 3, 2).reshape(g * 512, n)


def planes(y):
    n, m = y.shape
    v = y.astype(np.float32).astype(ml_dtypes.bfloat16).astype(np.float64).reshape(n // 32, 32, m)
    top = np.abs(v).max(1)
    byte = np.clip(np.where(top > 0, np.frexp(top)[1] - 1 + 127 - 7, 1), 1, 254)
    codes = (v * np.exp2(127.0 - byte)[:, None, :]).reshape(n, m).astype(np.float32).astype(ml_dtypes.float8_e4m3fn).view(np.uint8)
    words = codes.reshape(n // 512, 128, 4, m).transpose(0, 1, 3, 2)
    return np.ascontiguousarray(words), np.ascontiguousarray(byte.astype(np.uint8).reshape(n // 512, 16, m))


K, N, T, J = 512, 512, 2048, 512


def setup_inputs():
    n = np.random.standard_normal
    s = mx_kscale(K)[:, None]
    p_w = pack_weight(n((K, N)) / np.sqrt(K) / s, "e4m3")
    return {
        "xT": (n((K, T)) * s).astype(np.float32),
        "wgt": np.repeat(np.random.uniform(0.5, 2.0, (8, 2 * J)), 16, axis=0).astype(np.float32),
        "w_words": p_w[0],
        "w_scales": p_w[1],
        "res": (n((N, J))).astype(np.float32),
        "offs": striped8(np.stack([np.concatenate([np.random.permutation(T)[:J] for _ in range(2)]) for _ in range(8)])),
    }


def reference(xT, wgt, w_words, w_scales, res, offs):
    idx = unstriped8(offs)
    rows = np.arange(K)
    xg = f64(wgt)[rows // 4 % 128] * f64(xT)[rows[:, None], idx[rows % 512 // 64]]
    xT_ = mxq(xg, 0, "e4m3").reshape(K, 2, J)
    w_ = unpack_weight(w_words, w_scales, "e4m3")
    a0 = w_.T @ xT_[:, 0]
    a1 = w_.T @ xT_[:, 1]
    out_0 = f64(res) + np.maximum(a0, 0.0) + np.maximum(a1, 0.0)
    return (out_0,) + planes(out_0)

@@ -1,0 +1,158 @@
+from contextlib import ExitStack
+
+import concourse.mybir as mybir
+
+K, N, T, J = 512, 512, 2048, 512
+FLOPS = 2 * 2 * K * N * J
+
+F32 = mybir.dt.float32
+BF16 = mybir.dt.bfloat16
+I32 = mybir.dt.int32
+U32 = mybir.dt.uint32
+U16 = mybir.dt.uint16
+U8 = mybir.dt.uint8
+FP8X4 = mybir.dt.float8_e4m3fn_x4
+ALU = mybir.AluOpType
+
+P = 128
+PACK = 4
+PICKS = 2
+JC = 128
+CHUNKS = J // JC
+
+
+def tile_list_relus_resP_kernel(tc, xT, wgt, w_words, w_scales, res, offs, out_0, out_1, out_2):
+    nc = tc.nc
+    with ExitStack() as ctx:
+        keep = ctx.enter_context(tc.tile_pool(name="keep", bufs=1))
+        psum = ctx.enter_context(tc.psum_pool(name="psum", bufs=1))
+
+        offsets = keep.tile([P, PICKS * J // 16], U16, name="offsets")
+        nc.sync.dma_start(offsets[:], offs)
+
+        x_rows = xT.rearrange("(p i) t -> p i t", i=PACK)
+        x = [keep.tile([P, T], F32, name="x%d" % i) for i in range(PACK)]
+        wg = [keep.tile([P, J], F32, name="wg%d" % c) for c in range(PICKS)]
+        nc.sync.dma_start(wg[0][:], wgt[:, 0:J])
+        nc.sync.dma_start(x[0][:], x_rows[:, 0, :])
+        nc.sync.dma_start(wg[1][:], wgt[:, J : 2 * J])
+        for i in range(1, PACK):
+            nc.sync.dma_start(x[i][:], x_rows[:, i, :])
+
+        ws_raw = keep.tile([P, N], U8, name="ws_raw", align_bytes=64)
+        nc.vector.memset(ws_raw[:].bitcast(I32), 0)
+        for quad in range(4):
+            nc.scalar.dma_start(
+                ws_raw[32 * quad : 32 * quad + 4, :].bitcast(I32),
+                w_scales[0, 4 * quad : 4 * quad + 4, :].bitcast(I32),
+            )
+        ws = keep.tile([P, N], U8, name="ws", align_bytes=64)
+        nc.vector.tensor_copy(
+            out=ws[:].rearrange("p (t m) -> p t m", t=PACK),
+            in_=ws_raw[:].rearrange("p (m t) -> p t m", t=PACK),
+        )
+
+        wc_raw = keep.tile([P, N], I32, name="wc_raw", align_bytes=64)
+        nc.sync.dma_start(wc_raw[:], w_words[0].rearrange("p n i -> p (n i)").bitcast(I32))
+        res_rows = res.rearrange("(p t) j -> p t j", t=PACK)
+        res_sb = [keep.tile([P, PACK, J // 2], F32, name="res%d" % h) for h in range(2)]
+        for h in range(2):
+            nc.sync.dma_start(res_sb[h][:], res_rows[:, :, h * (J // 2) : (h + 1) * (J // 2)])
+
+        def gather(dst, i, c, j0, n):
+            col = (c * J + j0) // 16
+            nc.vector.tensor_tensor(dst, x[i][:].indirect(offsets[:, col : col + n // 16]), wg[c][:, j0 : j0 + n], ALU.mult)
+
+        g01 = [keep.tile([P, 2, J], F32, name="g01_%d" % c) for c in range(PICKS)]
+        g23 = [keep.tile([P, 2, PICKS, JC], F32, name="g23_%d" % q) for q in range(CHUNKS)]
+        xb = [keep.tile([P, PICKS, JC, PACK], BF16, name="xb%d" % q, align_bytes=64) for q in range(CHUNKS)]
+        for i in range(2):
+            for c in range(PICKS):
+                gather(g01[c][:, i, :], i, c, 0, J)
+        for c in range(PICKS):
+            for q in range(CHUNKS):
+                nc.scalar.copy(
+                    out=xb[q][:, c, :, 0:2].rearrange("p (a b) t -> p a t b", b=4),
+                    in_=g01[c][:, :, q * JC : (q + 1) * JC].rearrange("p t (a b) -> p a t b", b=4),
+                )
+        for q in range(CHUNKS):
+            for c in range(PICKS):
+                gather(g23[q][:, 0, c, :], 2, c, q * JC, JC)
+
+        wc = keep.tile([P, N], I32, name="wc", align_bytes=64)
+        xc = [keep.tile([P, PICKS * JC], U32, name="xc%d" % q, align_bytes=64) for q in range(CHUNKS)]
+        xs = [keep.tile([P, PICKS * JC], U8, name="xs%d" % q, align_bytes=64) for q in range(CHUNKS)]
+        acc = [[psum.tile([P, PACK, JC], F32, name="acc%d_%d" % (q, c)) for c in range(PICKS)] for q in range(CHUNKS)]
+        part = [keep.tile([P, PACK, JC], F32, name="part%d" % q) for q in range(CHUNKS)]
+        y = [keep.tile([P, PACK, JC], F32, name="y%d" % q) for q in range(CHUNKS)]
+        yb = [keep.tile([P, JC, PACK], BF16, name="yb%d" % q, align_bytes=64) for q in range(CHUNKS)]
+        yc = keep.tile([P, J], U32, name="yc", align_bytes=64)
+        ys = keep.tile([P, J], U8, name="ys", align_bytes=64)
+        out_rows = out_0.rearrange("(p t) j -> p t j", t=PACK)
+        out_words = out_1[0].rearrange("p j i -> p (j i)").bitcast(I32)
+
+        def last_plane(q):
+            for c in range(PICKS):
+                gather(g23[q][:, 1, c, :], 3, c, q * JC, JC)
+            nc.scalar.copy(
+                out=xb[q][:].rearrange("p c j t -> p (c j) t")[:, :, 2:4].rearrange("p (a b) t -> p a t b", b=4),
+                in_=g23[q][:].rearrange("p t c (a b) -> p (c a) t b", b=4),
+            )
+
+        def project(q):
+            nc.vector.quantize_mx(out=xc[q][:].bitcast(FP8X4), scales=xs[q][:], in_=xb[q][:].rearrange("p c j t -> p (c j t)"))
+            for c in range(PICKS):
+                cols = slice(c * JC, (c + 1) * JC)
+                for t in range(PACK):
+                    rows = slice(t * P, (t + 1) * P)
+                    nc.tensor.matmul_mx(
+                        out=acc[q][c][:, t, :],
+                        lhsT=wc[:, rows].bitcast(FP8X4),
+                        lhsT_scale=ws[:, rows],
+                        rhs=xc[q][:, cols].bitcast(FP8X4),
+                        rhs_scale=xs[q][:, cols],
+                        start=True,
+                        stop=True,
+                    )
+
+        def pool_picks(q):
+            h, r = divmod(q * JC, J // 2)
+            nc.vector.scalar_tensor_tensor(part[q][:], acc[q][0][:], 0.0, res_sb[h][:, :, r : r + JC], ALU.max, ALU.add)
+            nc.vector.scalar_tensor_tensor(y[q][:], acc[q][1][:], 0.0, part[q][:], ALU.max, ALU.add)
+            nc.sync.dma_start(out_rows[:, :, q * JC : (q + 1) * JC], y[q][:])
+            nc.scalar.copy(
+                out=yb[q][:].rearrange("p (a b) t -> p a t b", b=4),
+                in_=y[q][:].rearrange("p t (a b) -> p a t b", b=4),
+            )
+
+        def requantise(q):
+            cols = slice(q * JC, (q + 1) * JC)
+            nc.vector.quantize_mx(out=yc[:, cols].bitcast(FP8X4), scales=ys[:, cols], in_=yb[q][:].rearrange("p j t -> p (j t)"))
+            nc.sync.dma_start(out_words[:, cols], yc[:, cols].bitcast(I32))
+
+        last_plane(0)
+        last_plane(1)
+        nc.vector.tensor_copy(
+            out=wc[:].rearrange("p (t m) -> p t m", t=PACK),
+            in_=wc_raw[:].rearrange("p (m t) -> p t m", t=PACK),
+        )
+        project(0)
+        last_plane(2)
+        project(1)
+        last_plane(3)
+        pool_picks(0)
+        project(2)
+        pool_picks(1)
+        project(3)
+        requantise(0)
+        pool_picks(2)
+        requantise(1)
+        pool_picks(3)
+        requantise(2)
+        requantise(3)
+        for quad in range(4):
+            queue = nc.sync if quad % 2 else nc.scalar
+            queue.dma_start(
+                out_2[0, 4 * quad : 4 * quad + 4, :].bitcast(I32),
+                ys[32 * quad : 32 * quad + 4, :].bitcast(I32),
+            )

@@ -17,8 +17,11 @@ ALU = mybir.AluOpType
 P = 128
 PACK = 4
 PICKS = 2
-JC = 128
-CHUNKS = J // JC
+JH = 256
+JB = 128
+HALVES = J // JH
+BLOCKS = J // JB
+RELU = mybir.ActivationFunctionType.Relu
 
 
 def tile_list_relus_resP_kernel(tc, xT, wgt, w_words, w_scales, res, offs, out_0, out_1, out_2):
@@ -31,26 +34,25 @@ def tile_list_relus_resP_kernel(tc, xT, wgt, w_words, w_scales, res, offs, out_0
         nc.sync.dma_start(offsets[:], offs)
 
         x_rows = xT.rearrange("(p i) t -> p i t", i=PACK)
-        x = [keep.tile([P, T], F32, name="x%d" % i) for i in range(PACK)]
-        wg = [keep.tile([P, J], F32, name="wg%d" % c) for c in range(PICKS)]
-        nc.sync.dma_start(wg[0][:], wgt[:, 0:J])
+        x = [keep.tile([P, T], F32, name="x%d" % i, tag="x%d" % i, align_bytes=64) for i in range(PACK)]
+        ws_raw = keep.tile([P, N], U8, name="ws_raw", tag="early", align_bytes=64)
+        nc.gpsimd.memset(ws_raw[:].bitcast(I32), 0)
+        nc.sync.dma_start(ws_raw[0:16, :].bitcast(I32), w_scales[0].bitcast(I32))
+        wg = keep.tile([P, PICKS * J], F32, name="wg")
+        nc.sync.dma_start(wg[:, 0:JB], wgt[:, 0:JB])
         nc.sync.dma_start(x[0][:], x_rows[:, 0, :])
-        nc.sync.dma_start(wg[1][:], wgt[:, J : 2 * J])
+        nc.sync.dma_start(wg[:, JB:J], wgt[:, JB:J])
+        nc.sync.dma_start(wg[:, J : 2 * J], wgt[:, J : 2 * J])
         for i in range(1, PACK):
             nc.sync.dma_start(x[i][:], x_rows[:, i, :])
 
-        ws_raw = keep.tile([P, N], U8, name="ws_raw", align_bytes=64)
-        nc.vector.memset(ws_raw[:].bitcast(I32), 0)
-        for quad in range(4):
-            nc.scalar.dma_start(
-                ws_raw[32 * quad : 32 * quad + 4, :].bitcast(I32),
-                w_scales[0, 4 * quad : 4 * quad + 4, :].bitcast(I32),
-            )
         ws = keep.tile([P, N], U8, name="ws", align_bytes=64)
         nc.vector.tensor_copy(
             out=ws[:].rearrange("p (t m) -> p t m", t=PACK),
             in_=ws_raw[:].rearrange("p (m t) -> p t m", t=PACK),
         )
+        for quad in range(1, 4):
+            nc.scalar.dma_start(ws[32 * quad : 32 * quad + 4, :].bitcast(I32), ws[4 * quad : 4 * quad + 4, :].bitcast(I32))
 
         wc_raw = keep.tile([P, N], I32, name="wc_raw", align_bytes=64)
         nc.sync.dma_start(wc_raw[:], w_words[0].rearrange("p n i -> p (n i)").bitcast(I32))
@@ -61,95 +63,122 @@ def tile_list_relus_resP_kernel(tc, xT, wgt, w_words, w_scales, res, offs, out_0
 
         def gather(dst, i, c, j0, n):
             col = (c * J + j0) // 16
-            nc.vector.tensor_tensor(dst, x[i][:].indirect(offsets[:, col : col + n // 16]), wg[c][:, j0 : j0 + n], ALU.mult)
+            nc.vector.tensor_tensor(dst, x[i][:].indirect(offsets[:, col : col + n // 16]), wg[:, c * J + j0 : c * J + j0 + n], ALU.mult)
 
-        g01 = [keep.tile([P, 2, J], F32, name="g01_%d" % c) for c in range(PICKS)]
-        g23 = [keep.tile([P, 2, PICKS, JC], F32, name="g23_%d" % q) for q in range(CHUNKS)]
-        xb = [keep.tile([P, PICKS, JC, PACK], BF16, name="xb%d" % q, align_bytes=64) for q in range(CHUNKS)]
-        for i in range(2):
-            for c in range(PICKS):
-                gather(g01[c][:, i, :], i, c, 0, J)
+        g01 = [keep.tile([P, 2, J], F32, name="g01_%d" % c, tag="g01" if c else "early", align_bytes=64) for c in range(PICKS)]
+        steps = [(c, h) for c in range(PICKS) for h in range(HALVES)]
+        first, last = steps[0], steps[-1]
+        xb = {}
+        g23 = {}
+        for s in steps:
+            xb[s] = keep.tile([P, JH, PACK], BF16, name="xb%d%d" % s, tag="xb%d%d" % s, align_bytes=64)
+        for s in steps[:-1]:
+            g23[s] = keep.tile([P, 2, JH], F32, name="g23_%d%d" % s)
+        gather(g01[0][:, 0, 0:JB], 0, 0, 0, JB)
+        gather(g01[0][:, 0, JB:J], 0, 0, JB, J - JB)
+        gather(g01[1][:, 0, :], 0, 1, 0, J)
         for c in range(PICKS):
-            for q in range(CHUNKS):
+            gather(g01[c][:, 1, :], 1, c, 0, J)
+        for c in range(PICKS):
+            for h in range(HALVES):
                 nc.scalar.copy(
-                    out=xb[q][:, c, :, 0:2].rearrange("p (a b) t -> p a t b", b=4),
-                    in_=g01[c][:, :, q * JC : (q + 1) * JC].rearrange("p t (a b) -> p a t b", b=4),
+                    out=xb[c, h][:, :, 0:2].rearrange("p (a b) t -> p a t b", b=4),
+                    in_=g01[c][:, :, h * JH : (h + 1) * JH].rearrange("p t (a b) -> p a t b", b=4),
                 )
-        for q in range(CHUNKS):
-            for c in range(PICKS):
-                gather(g23[q][:, 0, c, :], 2, c, q * JC, JC)
+        for c, h in steps[:-1]:
+            gather(g23[c, h][:, 0, :], 2, c, h * JH, JH)
 
         wc = keep.tile([P, N], I32, name="wc", align_bytes=64)
-        xc = [keep.tile([P, PICKS * JC], U32, name="xc%d" % q, align_bytes=64) for q in range(CHUNKS)]
-        xs = [keep.tile([P, PICKS * JC], U8, name="xs%d" % q, align_bytes=64) for q in range(CHUNKS)]
-        acc = [[psum.tile([P, PACK, JC], F32, name="acc%d_%d" % (q, c)) for c in range(PICKS)] for q in range(CHUNKS)]
-        part = [keep.tile([P, PACK, JC], F32, name="part%d" % q) for q in range(CHUNKS)]
-        y = [keep.tile([P, PACK, JC], F32, name="y%d" % q) for q in range(CHUNKS)]
-        yb = [keep.tile([P, JC, PACK], BF16, name="yb%d" % q, align_bytes=64) for q in range(CHUNKS)]
+        xc = {s: keep.tile([P, JH], U32, name="xc%d%d" % s, align_bytes=64) for s in steps}
+        xs = {s: keep.tile([P, JH], U8, name="xs%d%d" % s, align_bytes=64) for s in steps}
+        acc = [[psum.tile([P, PACK, JB], F32, name="acc%d_%d" % (c, b)) for b in range(BLOCKS)] for c in range(PICKS)]
+        part = {b: keep.tile([P, PACK, JB], F32, name="part%d" % b) for b in (1, 2)}
+        relu = {b: keep.tile([P, PACK, JB], F32, name="relu%d" % b) for b in (0, 3)}
+        y01 = keep.tile([P, PACK, JH], F32, name="y01")
+        y = [y01[:, :, 0:JB], y01[:, :, JB:JH]] + [keep.tile([P, PACK, JB], F32, name="y%d" % b)[:] for b in (2, 3)]
+        yb = [keep.tile([P, JB, PACK], BF16, name="yb%d" % b, align_bytes=64) for b in range(BLOCKS)]
         yc = keep.tile([P, J], U32, name="yc", align_bytes=64)
         ys = keep.tile([P, J], U8, name="ys", align_bytes=64)
         out_rows = out_0.rearrange("(p t) j -> p t j", t=PACK)
         out_words = out_1[0].rearrange("p j i -> p (j i)").bitcast(I32)
 
-        def last_plane(q):
-            for c in range(PICKS):
-                gather(g23[q][:, 1, c, :], 3, c, q * JC, JC)
+        def last_plane(c, h):
+            gather(g23[c, h][:, 1, :], 3, c, h * JH, JH)
             nc.scalar.copy(
-                out=xb[q][:].rearrange("p c j t -> p (c j) t")[:, :, 2:4].rearrange("p (a b) t -> p a t b", b=4),
-                in_=g23[q][:].rearrange("p t c (a b) -> p (c a) t b", b=4),
+                out=xb[c, h][:, :, 2:4].rearrange("p (a b) t -> p a t b", b=4),
+                in_=g23[c, h][:].rearrange("p t (a b) -> p a t b", b=4),
             )
 
-        def project(q):
-            nc.vector.quantize_mx(out=xc[q][:].bitcast(FP8X4), scales=xs[q][:], in_=xb[q][:].rearrange("p c j t -> p (c j t)"))
-            for c in range(PICKS):
-                cols = slice(c * JC, (c + 1) * JC)
+        def project(c, h):
+            s = (c, h)
+            nc.vector.quantize_mx(out=xc[s][:].bitcast(FP8X4), scales=xs[s][:], in_=xb[s][:].rearrange("p j t -> p (j t)"))
+            for u in range(JH // JB):
+                cols = slice(u * JB, (u + 1) * JB)
                 for t in range(PACK):
                     rows = slice(t * P, (t + 1) * P)
                     nc.tensor.matmul_mx(
-                        out=acc[q][c][:, t, :],
+                        out=acc[c][h * (JH // JB) + u][:, t, :],
                         lhsT=wc[:, rows].bitcast(FP8X4),
                         lhsT_scale=ws[:, rows],
-                        rhs=xc[q][:, cols].bitcast(FP8X4),
-                        rhs_scale=xs[q][:, cols],
+                        rhs=xc[s][:, cols].bitcast(FP8X4),
+                        rhs_scale=xs[s][:, cols],
                         start=True,
                         stop=True,
                     )
 
-        def pool_picks(q):
-            h, r = divmod(q * JC, J // 2)
-            nc.vector.scalar_tensor_tensor(part[q][:], acc[q][0][:], 0.0, res_sb[h][:, :, r : r + JC], ALU.max, ALU.add)
-            nc.vector.scalar_tensor_tensor(y[q][:], acc[q][1][:], 0.0, part[q][:], ALU.max, ALU.add)
-            nc.sync.dma_start(out_rows[:, :, q * JC : (q + 1) * JC], y[q][:])
-            nc.scalar.copy(
-                out=yb[q][:].rearrange("p (a b) t -> p a t b", b=4),
-                in_=y[q][:].rearrange("p t (a b) -> p a t b", b=4),
+        def add_pick(c, b):
+            h, r = divmod(b * JB, JH)
+            if c == 0:
+                nc.vector.scalar_tensor_tensor(part[b][:], acc[0][b][:], 0.0, res_sb[h][:, :, r : r + JB], ALU.max, ALU.add)
+            else:
+                nc.vector.scalar_tensor_tensor(y[b], acc[1][b][:], 0.0, part[b][:], ALU.max, ALU.add)
+                if b == 1:
+                    nc.sync.dma_start(out_rows[:, :, 0:JH], y01[:])
+                elif b > 1:
+                    nc.sync.dma_start(out_rows[:, :, b * JB : (b + 1) * JB], y[b])
+
+        def add_res(b, tag, align):
+            h, r = divmod(b * JB, JH)
+            part[b] = keep.tile([P, PACK, JB], F32, name="part%d" % b, tag=tag, align_bytes=align)
+            nc.gpsimd.tensor_tensor(part[b][:], relu[b][:], res_sb[h][:, :, r : r + JB], ALU.add)
+
+        def round_y(b):
+            copy = nc.vector.tensor_copy if b == BLOCKS - 1 else nc.scalar.copy
+            copy(
+                out=yb[b][:].rearrange("p (a b) t -> p a t b", b=4),
+                in_=y[b].rearrange("p t (a b) -> p a t b", b=4),
             )
 
-        def requantise(q):
-            cols = slice(q * JC, (q + 1) * JC)
-            nc.vector.quantize_mx(out=yc[:, cols].bitcast(FP8X4), scales=ys[:, cols], in_=yb[q][:].rearrange("p j t -> p (j t)"))
-            nc.sync.dma_start(out_words[:, cols], yc[:, cols].bitcast(I32))
+        def requantise(b):
+            cols = slice(b * JB, (b + 1) * JB)
+            nc.vector.quantize_mx(out=yc[:, cols].bitcast(FP8X4), scales=ys[:, cols], in_=yb[b][:].rearrange("p j t -> p (j t)"))
 
-        last_plane(0)
-        last_plane(1)
+        last_plane(0, 0)
+        last_plane(0, 1)
+        last_plane(1, 0)
         nc.vector.tensor_copy(
             out=wc[:].rearrange("p (t m) -> p t m", t=PACK),
             in_=wc_raw[:].rearrange("p (m t) -> p t m", t=PACK),
         )
-        project(0)
-        last_plane(2)
-        project(1)
-        last_plane(3)
-        pool_picks(0)
-        project(2)
-        pool_picks(1)
-        project(3)
-        requantise(0)
-        pool_picks(2)
-        requantise(1)
-        pool_picks(3)
-        requantise(2)
-        requantise(3)
+        project(0, 0)
+        nc.scalar.activation(relu[0][:], acc[0][0][:], RELU)
+        project(0, 1)
+        nc.scalar.activation(relu[3][:], acc[0][3][:], RELU)
+        project(1, 0)
+        g23[last] = keep.tile([P, 2, JH], F32, name="g23_last", tag="xb00", align_bytes=64)
+        gather(g23[last][:, 0, :], 2, 1, JH, JH)
+        last_plane(1, 1)
+        add_res(0, "x3", 64)
+        add_pick(0, 1)
+        add_pick(0, 2)
+        project(1, 1)
+        add_res(3, "xb11", 64)
+        for b in range(BLOCKS):
+            add_pick(1, b)
+            round_y(b)
+        for b in range(BLOCKS):
+            requantise(b)
+        nc.sync.dma_start(out_words, yc[:].bitcast(I32))
         for quad in range(4):
             queue = nc.sync if quad % 2 else nc.scalar
             queue.dma_start(

@@ -82,8 +82,8 @@ def tile_list_relus_resP_kernel(tc, xT, wgt, w_words, w_scales, res, offs, out_0
         for c in range(PICKS):
             for h in range(HALVES):
                 nc.scalar.copy(
-                    out=xb[c, h][:, :, 0:2].rearrange("p (a b) t -> p a t b", b=4),
-                    in_=g01[c][:, :, h * JH : (h + 1) * JH].rearrange("p t (a b) -> p a t b", b=4),
+                    out=xb[c, h][:, :, 0:2],
+                    in_=g01[c][:, :, h * JH : (h + 1) * JH].rearrange("p t j -> p j t"),
                 )
         for c, h in steps[:-1]:
             gather(g23[c, h][:, 0, :], 2, c, h * JH, JH)
@@ -105,8 +105,8 @@ def tile_list_relus_resP_kernel(tc, xT, wgt, w_words, w_scales, res, offs, out_0
         def last_plane(c, h):
             gather(g23[c, h][:, 1, :], 3, c, h * JH, JH)
             nc.scalar.copy(
-                out=xb[c, h][:, :, 2:4].rearrange("p (a b) t -> p a t b", b=4),
-                in_=g23[c, h][:].rearrange("p t (a b) -> p a t b", b=4),
+                out=xb[c, h][:, :, 2:4],
+                in_=g23[c, h][:].rearrange("p t j -> p j t"),
             )
 
         def project(c, h):
@@ -157,8 +157,8 @@ def tile_list_relus_resP_kernel(tc, xT, wgt, w_words, w_scales, res, offs, out_0
         last_plane(0, 1)
         last_plane(1, 0)
         nc.vector.tensor_copy(
-            out=wc[:].rearrange("p (t m) -> p t m", t=PACK),
-            in_=wc_raw[:].rearrange("p (m t) -> p t m", t=PACK),
+            out=wc[:].rearrange("p (t m) -> p m t", t=PACK),
+            in_=wc_raw[:].rearrange("p (m t) -> p m t", t=PACK),
         )
         project(0, 0)
         nc.scalar.activation(relu[0][:], acc[0][0][:], RELU)

from contextlib import ExitStack

import concourse.mybir as mybir

K, N, T, J = 512, 512, 2048, 512
FLOPS = 2 * 2 * K * N * J

F32 = mybir.dt.float32
BF16 = mybir.dt.bfloat16
I32 = mybir.dt.int32
U32 = mybir.dt.uint32
U16 = mybir.dt.uint16
U8 = mybir.dt.uint8
FP8X4 = mybir.dt.float8_e4m3fn_x4
ALU = mybir.AluOpType

P = 128
PACK = 4
PICKS = 2
JH = 256
JB = 128
HALVES = J // JH
BLOCKS = J // JB
RELU = mybir.ActivationFunctionType.Relu


def tile_list_relus_resP_kernel(tc, xT, wgt, w_words, w_scales, res, offs, out_0, out_1, out_2):
    nc = tc.nc
    with ExitStack() as ctx:
        keep = ctx.enter_context(tc.tile_pool(name="keep", bufs=1))
        psum = ctx.enter_context(tc.psum_pool(name="psum", bufs=1))

        offsets = keep.tile([P, PICKS * J // 16], U16, name="offsets")
        nc.sync.dma_start(offsets[:], offs)

        x_rows = xT.rearrange("(p i) t -> p i t", i=PACK)
        x = [keep.tile([P, T], F32, name="x%d" % i, tag="x%d" % i, align_bytes=64) for i in range(PACK)]
        ws_raw = keep.tile([P, N], U8, name="ws_raw", tag="early", align_bytes=64)
        nc.gpsimd.memset(ws_raw[:].bitcast(I32), 0)
        nc.sync.dma_start(ws_raw[0:16, :].bitcast(I32), w_scales[0].bitcast(I32))
        wg = keep.tile([P, PICKS * J], F32, name="wg")
        nc.sync.dma_start(wg[:, 0:JB], wgt[:, 0:JB])
        nc.sync.dma_start(x[0][:], x_rows[:, 0, :])
        nc.sync.dma_start(wg[:, JB:J], wgt[:, JB:J])
        nc.sync.dma_start(wg[:, J : 2 * J], wgt[:, J : 2 * J])
        for i in range(1, PACK):
            nc.sync.dma_start(x[i][:], x_rows[:, i, :])

        ws = keep.tile([P, N], U8, name="ws", align_bytes=64)
        nc.vector.tensor_copy(
            out=ws[:].rearrange("p (t m) -> p t m", t=PACK),
            in_=ws_raw[:].rearrange("p (m t) -> p t m", t=PACK),
        )
        for quad in range(1, 4):
            nc.scalar.dma_start(ws[32 * quad : 32 * quad + 4, :].bitcast(I32), ws[4 * quad : 4 * quad + 4, :].bitcast(I32))

        wc_raw = keep.tile([P, N], I32, name="wc_raw", align_bytes=64)
        nc.sync.dma_start(wc_raw[:], w_words[0].rearrange("p n i -> p (n i)").bitcast(I32))
        res_rows = res.rearrange("(p t) j -> p t j", t=PACK)
        res_sb = [keep.tile([P, PACK, J // 2], F32, name="res%d" % h) for h in range(2)]
        for h in range(2):
            nc.sync.dma_start(res_sb[h][:], res_rows[:, :, h * (J // 2) : (h + 1) * (J // 2)])

        def gather(dst, i, c, j0, n):
            col = (c * J + j0) // 16
            nc.vector.tensor_tensor(dst, x[i][:].indirect(offsets[:, col : col + n // 16]), wg[:, c * J + j0 : c * J + j0 + n], ALU.mult)

        g01 = [keep.tile([P, 2, J], F32, name="g01_%d" % c, tag="g01" if c else "early", align_bytes=64) for c in range(PICKS)]
        steps = [(c, h) for c in range(PICKS) for h in range(HALVES)]
        first, last = steps[0], steps[-1]
        xb = {}
        g23 = {}
        for s in steps:
            xb[s] = keep.tile([P, JH, PACK], BF16, name="xb%d%d" % s, tag="xb%d%d" % s, align_bytes=64)
        for s in steps[:-1]:
            g23[s] = keep.tile([P, 2, JH], F32, name="g23_%d%d" % s)
        gather(g01[0][:, 0, 0:JB], 0, 0, 0, JB)
        gather(g01[0][:, 0, JB:J], 0, 0, JB, J - JB)
        gather(g01[1][:, 0, :], 0, 1, 0, J)
        for c in range(PICKS):
            gather(g01[c][:, 1, :], 1, c, 0, J)
        for c in range(PICKS):
            for h in range(HALVES):
                nc.scalar.copy(
                    out=xb[c, h][:, :, 0:2],
                    in_=g01[c][:, :, h * JH : (h + 1) * JH].rearrange("p t j -> p j t"),
                )
        for c, h in steps[:-1]:
            gather(g23[c, h][:, 0, :], 2, c, h * JH, JH)

        wc = keep.tile([P, N], I32, name="wc", align_bytes=64)
        xc = {s: keep.tile([P, JH], U32, name="xc%d%d" % s, align_bytes=64) for s in steps}
        xs = {s: keep.tile([P, JH], U8, name="xs%d%d" % s, align_bytes=64) for s in steps}
        acc = [[psum.tile([P, PACK, JB], F32, name="acc%d_%d" % (c, b)) for b in range(BLOCKS)] for c in range(PICKS)]
        part = {b: keep.tile([P, PACK, JB], F32, name="part%d" % b) for b in (1, 2)}
        relu = {b: keep.tile([P, PACK, JB], F32, name="relu%d" % b) for b in (0, 3)}
        y01 = keep.tile([P, PACK, JH], F32, name="y01")
        y = [y01[:, :, 0:JB], y01[:, :, JB:JH]] + [keep.tile([P, PACK, JB], F32, name="y%d" % b)[:] for b in (2, 3)]
        yb = [keep.tile([P, JB, PACK], BF16, name="yb%d" % b, align_bytes=64) for b in range(BLOCKS)]
        yc = keep.tile([P, J], U32, name="yc", align_bytes=64)
        ys = keep.tile([P, J], U8, name="ys", align_bytes=64)
        out_rows = out_0.rearrange("(p t) j -> p t j", t=PACK)
        out_words = out_1[0].rearrange("p j i -> p (j i)").bitcast(I32)

        def last_plane(c, h):
            gather(g23[c, h][:, 1, :], 3, c, h * JH, JH)
            nc.scalar.copy(
                out=xb[c, h][:, :, 2:4],
                in_=g23[c, h][:].rearrange("p t j -> p j t"),
            )

        def project(c, h):
            s = (c, h)
            nc.vector.quantize_mx(out=xc[s][:].bitcast(FP8X4), scales=xs[s][:], in_=xb[s][:].rearrange("p j t -> p (j t)"))
            for u in range(JH // JB):
                cols = slice(u * JB, (u + 1) * JB)
                for t in range(PACK):
                    rows = slice(t * P, (t + 1) * P)
                    nc.tensor.matmul_mx(
                        out=acc[c][h * (JH // JB) + u][:, t, :],
                        lhsT=wc[:, rows].bitcast(FP8X4),
                        lhsT_scale=ws[:, rows],
                        rhs=xc[s][:, cols].bitcast(FP8X4),
                        rhs_scale=xs[s][:, cols],
                        start=True,
                        stop=True,
                    )

        def add_pick(c, b):
            h, r = divmod(b * JB, JH)
            if c == 0:
                nc.vector.scalar_tensor_tensor(part[b][:], acc[0][b][:], 0.0, res_sb[h][:, :, r : r + JB], ALU.max, ALU.add)
            else:
                nc.vector.scalar_tensor_tensor(y[b], acc[1][b][:], 0.0, part[b][:], ALU.max, ALU.add)
                if b == 1:
                    nc.sync.dma_start(out_rows[:, :, 0:JH], y01[:])
                elif b > 1:
                    nc.sync.dma_start(out_rows[:, :, b * JB : (b + 1) * JB], y[b])

        def add_res(b, tag, align):
            h, r = divmod(b * JB, JH)
            part[b] = keep.tile([P, PACK, JB], F32, name="part%d" % b, tag=tag, align_bytes=align)
            nc.gpsimd.tensor_tensor(part[b][:], relu[b][:], res_sb[h][:, :, r : r + JB], ALU.add)

        def round_y(b):
            copy = nc.vector.tensor_copy if b == BLOCKS - 1 else nc.scalar.copy
            copy(
                out=yb[b][:].rearrange("p (a b) t -> p a t b", b=4),
                in_=y[b].rearrange("p t (a b) -> p a t b", b=4),
            )

        def requantise(b):
            cols = slice(b * JB, (b + 1) * JB)
            nc.vector.quantize_mx(out=yc[:, cols].bitcast(FP8X4), scales=ys[:, cols], in_=yb[b][:].rearrange("p j t -> p (j t)"))

        last_plane(0, 0)
        last_plane(0, 1)
        last_plane(1, 0)
        nc.vector.tensor_copy(
            out=wc[:].rearrange("p (t m) -> p m t", t=PACK),
            in_=wc_raw[:].rearrange("p (m t) -> p m t", t=PACK),
        )
        project(0, 0)
        nc.scalar.activation(relu[0][:], acc[0][0][:], RELU)
        project(0, 1)
        nc.scalar.activation(relu[3][:], acc[0][3][:], RELU)
        project(1, 0)
        g23[last] = keep.tile([P, 2, JH], F32, name="g23_last", tag="xb00", align_bytes=64)
        gather(g23[last][:, 0, :], 2, 1, JH, JH)
        last_plane(1, 1)
        add_res(0, "x3", 64)
        add_pick(0, 1)
        add_pick(0, 2)
        project(1, 1)
        add_res(3, "xb11", 64)
        for b in range(BLOCKS):
            add_pick(1, b)
            round_y(b)
        for b in range(BLOCKS):
            requantise(b)
        nc.sync.dma_start(out_words, yc[:].bitcast(I32))
        for quad in range(4):
            queue = nc.sync if quad % 2 else nc.scalar
            queue.dma_start(
                out_2[0, 4 * quad : 4 * quad + 4, :].bitcast(I32),
                ys[32 * quad : 32 * quad + 4, :].bitcast(I32),
            )
